import numpy as np
import ml_dtypes


def mxq(x, axis, fmt="e4m3"):
    dtype, down = {"e4m3": (ml_dtypes.float8_e4m3fn, 7), "e5m2": (ml_dtypes.float8_e5m2, 14)}[fmt]
    v = np.moveaxis(np.asarray(x, np.float32).astype(ml_dtypes.bfloat16).astype(np.float64), axis, -1)
    blocks = v.reshape(v.shape[:-1] + (-1, 32))
    amax = np.abs(blocks).max(-1, keepdims=True)
    byte = np.maximum(np.where(amax > 0, np.frexp(amax)[1] - 1 + 127, 0) - down, 1)
    scale = np.exp2(byte - 127.0)
    codes = (blocks / scale).astype(np.float32).astype(dtype).astype(np.float64)
    return np.moveaxis((codes * scale).reshape(v.shape), -1, axis)


WIDE = False


def mx_kscale(k):
    if not WIDE:
        return np.ones(k)
    levels = np.array([10, -10, 5, -5, 0])
    if k % 512:
        return np.exp2(np.random.permutation(np.resize(levels, k // 32))).repeat(32)
    a = np.empty((k // 512, 16))
    for p in range(k // 512):
        a[p, :8] = np.random.permutation(np.resize(levels, 8))
        for g in range(8):
            far = levels[np.abs(levels - a[p, g]) >= 10]
            a[p, g + 8] = far[np.random.randint(len(far))]
    return np.exp2(a.ravel()).repeat(32)


def f64(x):
    return np.asarray(x).astype(np.float64)


def striped(idx):
    return np.tile(np.asarray(idx).reshape(-1, 16).T, (8, 1)).astype(np.uint16)


def unstriped(offs):
    return offs[:16].T.reshape(-1).astype(np.int64)


E2M1 = np.array([0.0, 0.5, 1.0, 1.5, 2.0, 3.0, 4.0, 6.0, -0.0, -0.5, -1.0, -1.5, -2.0, -3.0, -4.0, -6.0])


def pack_weight(w, fmt):
    k, n = w.shape
    w = f64(np.asarray(w, np.float32).astype(ml_dtypes.bfloat16)).reshape(k // 32, 32, n)
    amax = np.abs(w).max(1)
    if fmt == "e4m3":
        byte = np.frexp(amax)[1] - 1 + 127 - 7
    else:
        mant, ex = np.frexp(amax / 6.0)
        byte = np.where(mant > 0.5, ex, ex - 1) + 127
    byte = np.clip(np.where(amax > 0, byte, 1), 1, 254)
    scaled = (w * np.exp2(127.0 - byte)[:, None, :]).reshape(k, n).astype(np.float32)
    by_word = np.ascontiguousarray(scaled.reshape(k // 512, 128, 4, n).transpose(0, 1, 3, 2))
    if fmt == "e4m3":
        words = by_word.astype(ml_dtypes.float8_e4m3fn).view(np.uint8)
    else:
        c = by_word.astype(ml_dtypes.float4_e2m1fn).view(np.uint8) & 0xF
        words = (c[..., 0::2] | (c[..., 1::2] << 4)).reshape(k // 512, 128, 2 * n)
    return np.ascontiguousarray(words), np.ascontiguousarray(byte.astype(np.uint8).reshape(k // 512, 16, n))


def unpack_weight(words, scales, fmt):
    g, _, n = scales.shape
    words = np.ascontiguousarray(words).reshape(g, 128, n, -1)
    if fmt == "e4m3":
        vals = words.view(ml_dtypes.float8_e4m3fn).astype(np.float64)
    else:
        nib = np.empty((g, 128, n, 4), np.uint8)
        nib[..., 0::2] = words & 0xF
        nib[..., 1::2] = words >> 4
        vals = E2M1[nib]
    vals = vals * np.repeat(np.exp2(scales.astype(np.float64) - 127.0), 8, axis=1)[..., None]
    return vals.transpose(0, 1, 3, 2).reshape(g * 512, n)


def bf(x):
    return np.asarray(x, np.float32).astype(ml_dtypes.bfloat16)


def planes(Y):
    r, m = Y.shape
    b = f64(bf(Y)).reshape(r // 32, 32, m)
    amax = np.abs(b).max(1)
    byte = np.clip(np.where(amax > 0, np.frexp(amax)[1] - 1 + 127 - 7, 1), 1, 254)
    codes = (b * np.exp2(127.0 - byte)[:, None, :]).reshape(r, m).astype(np.float32).astype(ml_dtypes.float8_e4m3fn).view(np.uint8)
    words = codes.reshape(r // 512, 128, 4, m).transpose(0, 1, 3, 2)
    return np.ascontiguousarray(words), np.ascontiguousarray(byte.astype(np.uint8).reshape(r // 512, 16, m))


D, T, I, Q, E = 512, 2048, 512, 256, 512


def setup_inputs():
    n = np.random.standard_normal
    idx = np.random.permutation(T)[:I]
    fd = mx_kscale(D)
    fi = mx_kscale(I)
    ti = np.ones(T)
    ti[idx] = fi
    keysp = pack_weight(n((D, T)) / fd[:, None], "e2m1")
    return {
        "query": (n((D, Q)) * 0.8 / np.sqrt(D) * fd[:, None]).astype(np.float32),
        "keys_words": keysp[0],
        "keys_scales": keysp[1],
        "prior": np.tile(np.random.uniform(0.5, 1.5, T) / 512, (128, 1)).astype(np.float32),
        "size": (np.random.uniform(4.0, 16.0, (1, I)) * fi).astype(np.float32),
        "vals": (n((E, T)) / ti).astype(np.float32),
        "offs": striped(idx),
    }


def reference(query, keys_words, keys_scales, prior, size, vals, offs):
    idx = unstriped(offs)
    keysu = unpack_weight(keys_words, keys_scales, "e2m1")
    queryq = mxq(f64(query), 0, "e4m3")
    keysidxg = keysu[:, idx]
    a = queryq.T @ keysidxg
    p = np.exp(a - np.max(a, axis=1, keepdims=True))
    w = (p / np.sum(p, axis=1, keepdims=True) - f64(prior)[:1][:, idx]) * f64(size)
    wt = w.T
    vt = f64(vals)[:, idx].T
    vtq = mxq(vt, 0, "e4m3")
    wtq = mxq(wt, 0, "e4m3")
    o = vtq.T @ wtq
    words, scales = planes(o)
    return o, words, scales

@@ -1,0 +1,194 @@
+from contextlib import ExitStack
+
+import concourse.mybir as mybir
+from concourse.masks import make_identity
+
+D, T, I, Q, E = 512, 2048, 512, 256, 512
+P = 128
+PACK = 4
+HALVES = Q // P
+FLOPS = 2 * D * I * Q + 2 * I * E * Q
+BYTES = 4 * D * Q + D * T // 2 + D * T // 32 + 4 * T + 4 * I + 4 * E * T + 2 * P * I // 16 + 4 * E * Q + E * Q + E * Q // 32
+
+F32 = mybir.dt.float32
+BF16 = mybir.dt.bfloat16
+I32 = mybir.dt.int32
+U32 = mybir.dt.uint32
+U16 = mybir.dt.uint16
+U8 = mybir.dt.uint8
+FP8X4 = mybir.dt.float8_e4m3fn_x4
+FP4X4 = mybir.dt.float4_e2m1fn_x4
+ALU = mybir.AluOpType
+ACT = mybir.ActivationFunctionType
+AX = mybir.AxisListType
+
+LAST_ON_VECTOR = 320
+
+
+def tile_attend_overaverage_pl_kernel(tc, query, keys_words, keys_scales, prior, size, vals, offs, out_0, out_1, out_2):
+    nc = tc.nc
+    with ExitStack() as ctx:
+        sb = ctx.enter_context(tc.tile_pool(name="sb", bufs=1))
+        ps = ctx.enter_context(tc.psum_pool(name="ps", bufs=1))
+
+        offsets = sb.tile([P, I // 16], U16, name="offsets")
+        nc.sync.dma_start(offsets[:], offs)
+
+        key_words = sb.tile([P, T], U16, name="key_words", align_bytes=64)
+        nc.sync.dma_start(key_words[:].bitcast(I32), keys_words[0].bitcast(I32))
+        key_bytes = sb.tile([P, T], U8, name="key_bytes", align_bytes=64)
+        nc.vector.memset(key_bytes[:].bitcast(I32), 0)
+        for quad in range(4):
+            nc.scalar.dma_start(
+                key_bytes[32 * quad : 32 * quad + 4, :].bitcast(I32),
+                keys_scales[0, 4 * quad : 4 * quad + 4, :].bitcast(I32),
+            )
+        query_raw = sb.tile([P, PACK, Q], F32, name="query_raw")
+        nc.sync.dma_start(query_raw[:], query.rearrange("(p t) q -> p t q", t=PACK))
+        prior_pool = sb.tile([P, T], F32, name="prior_pool")
+        nc.vector.memset(prior_pool[0 : P - 1, :], 0.0)
+        nc.scalar.dma_start(prior_pool[P - 1 : P, :], prior[0:1, :])
+        size_col = sb.tile([P, PACK], F32, name="size_col")
+        nc.scalar.dma_start(size_col[:], size.rearrange("o (s r) -> (o s) r", r=PACK))
+        vals_dealt = vals.rearrange("(p j) t -> j p t", j=PACK)
+        val_pool = [sb.tile([P, T], F32, name=f"val_pool{j}") for j in range(PACK)]
+        for j in range(PACK):
+            nc.sync.dma_start(val_pool[j][:], vals_dealt[j])
+
+        ident = sb.tile([P, P], F32, name="ident")
+        make_identity(nc, ident[:])
+
+        key_words_g = sb.tile([P, I], U16, name="key_words_g", align_bytes=64)
+        nc.vector.tensor_copy(key_words_g[:], key_words[:].indirect(offsets[:]))
+        key_bytes_g = sb.tile([P, I], U8, name="key_bytes_g", align_bytes=64)
+        nc.vector.tensor_copy(key_bytes_g[:], key_bytes[:].indirect(offsets[:]))
+
+        query_bf = sb.tile([P, Q * PACK], BF16, name="query_bf", align_bytes=64)
+        nc.scalar.activation(
+            query_bf[:].rearrange("p (c i t) -> p c t i", i=4, t=PACK),
+            query_raw[:].rearrange("p t (c i) -> p c t i", i=4),
+            ACT.Copy,
+        )
+        query_codes = sb.tile([P, Q], U32, name="query_codes", align_bytes=64)
+        query_scales = sb.tile([P, Q], U8, name="query_scales", align_bytes=64)
+        nc.vector.quantize_mx(query_codes[:].bitcast(FP8X4), query_scales[:], query_bf[:])
+
+        scores = [ps.tile([P, I], F32, name=f"scores{h}", tag=f"rows{h}") for h in range(HALVES)]
+        for h in range(HALVES):
+            cols = slice(h * P, (h + 1) * P)
+            nc.tensor.matmul_mx(
+                scores[h][:],
+                lhsT=query_codes[:, cols].bitcast(FP8X4),
+                lhsT_scale=query_scales[:, cols],
+                rhs=key_words_g[:].bitcast(FP4X4),
+                rhs_scale=key_bytes_g[:],
+                start=True,
+                stop=True,
+            )
+
+        size_rows = ps.tile([P, PACK, P], F32, name="size_rows")
+        for r in range(PACK):
+            nc.tensor.transpose(size_rows[:, r, :], size_col[:, r : r + 1].to_broadcast([P, P]), ident[:])
+
+        neg_max = [sb.tile([P, 1], F32, name=f"neg_max{h}") for h in range(HALVES)]
+        row_sum = [sb.tile([P, 1], F32, name=f"row_sum{h}") for h in range(HALVES)]
+        row_inv = [sb.tile([P, 1], F32, name=f"row_inv{h}") for h in range(HALVES)]
+        probs = [sb.tile([P, I], F32, name=f"probs{h}") for h in range(HALVES)]
+        sized = [sb.tile([P, I], F32, name=f"sized{h}") for h in range(HALVES)]
+        for h in range(HALVES):
+            nc.vector.tensor_reduce(neg_max[h][:], scores[h][:], AX.X, ALU.max, negate=True)
+            nc.scalar.activation(
+                probs[h][:].rearrange("q (r s) -> q r s", r=PACK),
+                scores[h][:].rearrange("q (s r) -> q r s", r=PACK),
+                ACT.Exp,
+                bias=neg_max[h][:],
+                scale=1.0,
+                accum_out=row_sum[h][:],
+            )
+
+        prior_g = sb.tile([P, I], F32, name="prior_g")
+        nc.vector.tensor_copy(prior_g[:], prior_pool[:].indirect(offsets[:]))
+        prior_t = ps.tile([P, PACK, P], F32, name="prior_t")
+        for r in range(PACK):
+            nc.tensor.transpose(prior_t[:, r, :], prior_g[:, r::PACK], ident[:])
+        prior_sized = sb.tile([P, PACK], F32, name="prior_sized")
+        nc.vector.tensor_tensor(prior_sized[:], prior_t[:, :, P - 1], size_col[:], ALU.mult)
+
+        weight_bf = sb.tile([P, Q * PACK], BF16, name="weight_bf", align_bytes=64)
+        for h in range(HALVES):
+            nc.vector.reciprocal(row_inv[h][:], row_sum[h][:])
+            nc.vector.scalar_tensor_tensor(
+                sized[h][:], probs[h][:], row_inv[h][:], size_rows[:].rearrange("q r s -> q (r s)"), ALU.mult, ALU.mult
+            )
+        for h in range(HALVES):
+            sized_t = ps.tile([P, PACK, P], F32, name=f"sized_t{h}", tag=f"rows{h}")
+            for r in range(PACK):
+                nc.tensor.transpose(sized_t[:, r, :], sized[h][:, r * P : (r + 1) * P], ident[:])
+            nc.vector.tensor_tensor(
+                weight_bf[:, h * P * PACK : (h + 1) * P * PACK].rearrange("s (q r) -> s q r", r=PACK),
+                sized_t[:].rearrange("s r q -> s q r"),
+                prior_sized[:].unsqueeze(1).broadcast_to([P, P, PACK]),
+                ALU.subtract,
+            )
+        weight_codes = sb.tile([P, Q], U32, name="weight_codes", align_bytes=64)
+        weight_scales = sb.tile([P, Q], U8, name="weight_scales", align_bytes=64)
+        nc.vector.quantize_mx(weight_codes[:].bitcast(FP8X4), weight_scales[:], weight_bf[:])
+
+        result = [ps.tile([P, PACK, P], F32, name=f"result{h}") for h in range(HALVES)]
+        for j in range(PACK):
+            val_g = sb.tile([P, I], BF16, name=f"val_g{j}", align_bytes=64)
+            if j < 2:
+                nc.scalar.activation(val_g[:], val_pool[j][:].indirect(offsets[:]), ACT.Copy)
+            elif j == 2:
+                nc.vector.tensor_copy(val_g[:], val_pool[j][:].indirect(offsets[:]))
+            else:
+                cut = LAST_ON_VECTOR
+                nc.vector.tensor_copy(val_g[:, :cut], val_pool[j][:].indirect(offsets[:, : cut // 16]))
+                nc.scalar.activation(val_g[:, cut:], val_pool[j][:].indirect(offsets[:, cut // 16 :]), ACT.Copy)
+            val_t = ps.tile([P, 2, P], F32, name=f"val_t{j}", tag=f"val_t{j % 2}")
+            pairs = val_g[:].bitcast(F32)
+            for u in range(2):
+                nc.tensor.transpose(val_t[:, u, :], pairs[:, u::2], ident[:])
+            val_bf = sb.tile([P, P * PACK], BF16, name=f"val_bf{j}", align_bytes=64)
+            nc.scalar.copy(
+                val_bf[:].bitcast(F32).rearrange("s (e u) -> s e u", u=2), val_t[:].rearrange("s u e -> s e u")
+            )
+            val_codes = sb.tile([P, P], U32, name=f"val_codes{j}", align_bytes=64)
+            val_scales = sb.tile([P, P], U8, name=f"val_scales{j}", align_bytes=64)
+            nc.vector.quantize_mx(val_codes[:].bitcast(FP8X4), val_scales[:], val_bf[:])
+            for h in range(HALVES):
+                cols = slice(h * P, (h + 1) * P)
+                nc.tensor.matmul_mx(
+                    result[h][:, j, :],
+                    lhsT=val_codes[:].bitcast(FP8X4),
+                    lhsT_scale=val_scales[:],
+                    rhs=weight_codes[:, cols].bitcast(FP8X4),
+                    rhs_scale=weight_scales[:, cols],
+                    start=True,
+                    stop=True,
+                )
+            if j == PACK - 2:
+                out_early = sb.tile([P, PACK - 1, Q], F32, name="out_early")
+                for h in range(HALVES):
+                    nc.scalar.copy(out_early[:, :, h * P : (h + 1) * P], result[h][:, 0 : PACK - 1, :])
+                nc.sync.dma_start(out_0.rearrange("(p j) q -> p j q", j=PACK)[:, 0 : PACK - 1, :], out_early[:])
+
+        out_bf = [sb.tile([P, P * PACK], BF16, name=f"out_bf{h}", align_bytes=64) for h in range(HALVES)]
+        nc.scalar.copy(out_bf[0][:].rearrange("e (q j) -> e q j", j=PACK), result[0][:].rearrange("e j q -> e q j"))
+        nc.vector.tensor_copy(out_bf[1][:].rearrange("e (q j) -> e q j", j=PACK), result[1][:].rearrange("e j q -> e q j"))
+        out_codes = sb.tile([P, Q], U32, name="out_codes", align_bytes=64)
+        out_scales = sb.tile([P, Q], U8, name="out_scales", align_bytes=64)
+        for h in range(HALVES):
+            cols = slice(h * P, (h + 1) * P)
+            nc.vector.quantize_mx(out_codes[:, cols].bitcast(FP8X4), out_scales[:, cols], out_bf[h][:])
+        out_last = sb.tile([P, Q], F32, name="out_last")
+        for h in range(HALVES):
+            nc.scalar.copy(out_last[:, h * P : (h + 1) * P], result[h][:, PACK - 1, :])
+        nc.scalar.dma_start(out_0.rearrange("(p j) q -> p j q", j=PACK)[:, PACK - 1, :], out_last[:])
+        nc.sync.dma_start(out_1[0].rearrange("p c r -> p (c r)").bitcast(I32), out_codes[:].bitcast(I32))
+        for quad in range(4):
+            queue = nc.sync if quad < 2 else nc.scalar
+            queue.dma_start(
+                out_2[0, 4 * quad : 4 * quad + 4, :].bitcast(I32),
+                out_scales[32 * quad : 32 * quad + 4, :].bitcast(I32),
+            )

@@ -1,7 +1,6 @@
 from contextlib import ExitStack
 
 import concourse.mybir as mybir
-from concourse.masks import make_identity
 
 D, T, I, Q, E = 512, 2048, 512, 256, 512
 P = 128
@@ -22,22 +21,28 @@ ALU = mybir.AluOpType
 ACT = mybir.ActivationFunctionType
 AX = mybir.AxisListType
 
-LAST_ON_VECTOR = 320
+EARLY = 2
 
 
 def tile_attend_overaverage_pl_kernel(tc, query, keys_words, keys_scales, prior, size, vals, offs, out_0, out_1, out_2):
     nc = tc.nc
     with ExitStack() as ctx:
         sb = ctx.enter_context(tc.tile_pool(name="sb", bufs=1))
+        reused = ctx.enter_context(tc.tile_pool(name="reused", bufs=1))
         ps = ctx.enter_context(tc.psum_pool(name="ps", bufs=1))
 
         offsets = sb.tile([P, I // 16], U16, name="offsets")
         nc.sync.dma_start(offsets[:], offs)
 
-        key_words = sb.tile([P, T], U16, name="key_words", align_bytes=64)
+        key_bytes = reused.tile([P, T], U8, name="key_bytes", offset=8256, align_bytes=64)
+        nc.gpsimd.memset(key_bytes[:].bitcast(I32), 0)
+        prior_pool = sb.tile([P, T], F32, name="prior_pool", tag="wide1", align_bytes=64)
+        nc.vector.memset(prior_pool[0 : P - 1, :], 0.0)
+        nc.scalar.dma_start(prior_pool[P - 1 : P, :], prior[0:1, :])
+        size_col = sb.tile([P, PACK], F32, name="size_col")
+        nc.scalar.dma_start(size_col[:], size.rearrange("o (s r) -> (o s) r", r=PACK))
+        key_words = sb.tile([P, T], U16, name="key_words", tag="wide2", align_bytes=64)
         nc.sync.dma_start(key_words[:].bitcast(I32), keys_words[0].bitcast(I32))
-        key_bytes = sb.tile([P, T], U8, name="key_bytes", align_bytes=64)
-        nc.vector.memset(key_bytes[:].bitcast(I32), 0)
         for quad in range(4):
             nc.scalar.dma_start(
                 key_bytes[32 * quad : 32 * quad + 4, :].bitcast(I32),
@@ -45,37 +50,40 @@ def tile_attend_overaverage_pl_kernel(tc, query, keys_words, keys_scales, prior,
             )
         query_raw = sb.tile([P, PACK, Q], F32, name="query_raw")
         nc.sync.dma_start(query_raw[:], query.rearrange("(p t) q -> p t q", t=PACK))
-        prior_pool = sb.tile([P, T], F32, name="prior_pool")
-        nc.vector.memset(prior_pool[0 : P - 1, :], 0.0)
-        nc.scalar.dma_start(prior_pool[P - 1 : P, :], prior[0:1, :])
-        size_col = sb.tile([P, PACK], F32, name="size_col")
-        nc.scalar.dma_start(size_col[:], size.rearrange("o (s r) -> (o s) r", r=PACK))
-        vals_dealt = vals.rearrange("(p j) t -> j p t", j=PACK)
-        val_pool = [sb.tile([P, T], F32, name=f"val_pool{j}") for j in range(PACK)]
-        for j in range(PACK):
-            nc.sync.dma_start(val_pool[j][:], vals_dealt[j])
 
+        zeros = reused.tile([P, P], F32, name="zeros", offset=0)
+        nc.gpsimd.memset(zeros[:], 0.0)
         ident = sb.tile([P, P], F32, name="ident")
-        make_identity(nc, ident[:])
+        nc.gpsimd.affine_select(
+            out=ident[:], in_=zeros[:], compare_op=ALU.not_equal, fill=1.0, base=0, pattern=[[-1, P]], channel_multiplier=1
+        )
+
+
+        size_rows = ps.tile([P, PACK, P], F32, name="size_rows", tag="bank3")
+        for r in range(PACK):
+            nc.tensor.transpose(size_rows[:, r, :], size_col[:, r : r + 1].to_broadcast([P, P]), ident[:])
+        prior_g = sb.tile([P, I], F32, name="prior_g")
+        nc.vector.tensor_copy(prior_g[:], prior_pool[:].indirect(offsets[:]))
+        prior_t = ps.tile([P, PACK, P], F32, name="prior_t", tag="bank2")
+        for r in range(PACK):
+            nc.tensor.transpose(prior_t[:, r, :], prior_g[:, r::PACK], ident[:])
 
         key_words_g = sb.tile([P, I], U16, name="key_words_g", align_bytes=64)
         nc.vector.tensor_copy(key_words_g[:], key_words[:].indirect(offsets[:]))
         key_bytes_g = sb.tile([P, I], U8, name="key_bytes_g", align_bytes=64)
         nc.vector.tensor_copy(key_bytes_g[:], key_bytes[:].indirect(offsets[:]))
 
-        query_bf = sb.tile([P, Q * PACK], BF16, name="query_bf", align_bytes=64)
-        nc.scalar.activation(
-            query_bf[:].rearrange("p (c i t) -> p c t i", i=4, t=PACK),
-            query_raw[:].rearrange("p t (c i) -> p c t i", i=4),
-            ACT.Copy,
-        )
-        query_codes = sb.tile([P, Q], U32, name="query_codes", align_bytes=64)
+        query_codes = reused.tile([P, Q], U32, name="query_codes", offset=8256, align_bytes=64)
         query_scales = sb.tile([P, Q], U8, name="query_scales", align_bytes=64)
-        nc.vector.quantize_mx(query_codes[:].bitcast(FP8X4), query_scales[:], query_bf[:])
-
-        scores = [ps.tile([P, I], F32, name=f"scores{h}", tag=f"rows{h}") for h in range(HALVES)]
+        query_bf = [sb.tile([P, P * PACK], BF16, name=f"query_bf{h}", tag=f"query_bf{h}", align_bytes=64) for h in range(HALVES)]
+        for h in range(HALVES):
+            woven = query_bf[h][:].rearrange("p (c i t) -> p c t i", i=4, t=PACK)
+            rows = query_raw[:, :, h * P : (h + 1) * P].rearrange("p t (c i) -> p c t i", i=4)
+            nc.scalar.activation(woven, rows, ACT.Copy)
+        scores = [ps.tile([P, I], F32, name=f"scores{h}", tag=f"bank{h}") for h in range(HALVES)]
         for h in range(HALVES):
             cols = slice(h * P, (h + 1) * P)
+            nc.vector.quantize_mx(query_codes[:, cols].bitcast(FP8X4), query_scales[:, cols], query_bf[h][:])
             nc.tensor.matmul_mx(
                 scores[h][:],
                 lhsT=query_codes[:, cols].bitcast(FP8X4),
@@ -86,14 +94,20 @@ def tile_attend_overaverage_pl_kernel(tc, query, keys_words, keys_scales, prior,
                 stop=True,
             )
 
-        size_rows = ps.tile([P, PACK, P], F32, name="size_rows")
-        for r in range(PACK):
-            nc.tensor.transpose(size_rows[:, r, :], size_col[:, r : r + 1].to_broadcast([P, P]), ident[:])
+        vals_dealt = vals.rearrange("(p j) t -> j p t", j=PACK)
+        val_pool = [
+            reused.tile([P, T], F32, name="val_pool0", offset=64),
+            sb.tile([P, T], F32, name="val_pool1", tag="wide1", align_bytes=64),
+            sb.tile([P, T], F32, name="val_pool2", tag="wide2", align_bytes=64),
+            reused.tile([P, T], F32, name="val_pool3", offset=9280),
+        ]
+        for j in range(PACK):
+            nc.sync.dma_start(val_pool[j][:], vals_dealt[j])
 
-        neg_max = [sb.tile([P, 1], F32, name=f"neg_max{h}") for h in range(HALVES)]
+        neg_max = [sb.tile([P, 1], F32, name="neg_max0"), sb.tile([P, 1], F32, name="neg_max1", tag="val_g1", align_bytes=64)]
         row_sum = [sb.tile([P, 1], F32, name=f"row_sum{h}") for h in range(HALVES)]
         row_inv = [sb.tile([P, 1], F32, name=f"row_inv{h}") for h in range(HALVES)]
-        probs = [sb.tile([P, I], F32, name=f"probs{h}") for h in range(HALVES)]
+        probs = [sb.tile([P, I], F32, name=f"probs{h}", tag=f"probs{h}", align_bytes=64) for h in range(HALVES)]
         sized = [sb.tile([P, I], F32, name=f"sized{h}") for h in range(HALVES)]
         for h in range(HALVES):
             nc.vector.tensor_reduce(neg_max[h][:], scores[h][:], AX.X, ALU.max, negate=True)
@@ -106,56 +120,63 @@ def tile_attend_overaverage_pl_kernel(tc, query, keys_words, keys_scales, prior,
                 accum_out=row_sum[h][:],
             )
 
-        prior_g = sb.tile([P, I], F32, name="prior_g")
-        nc.vector.tensor_copy(prior_g[:], prior_pool[:].indirect(offsets[:]))
-        prior_t = ps.tile([P, PACK, P], F32, name="prior_t")
-        for r in range(PACK):
-            nc.tensor.transpose(prior_t[:, r, :], prior_g[:, r::PACK], ident[:])
-        prior_sized = sb.tile([P, PACK], F32, name="prior_sized")
+        prior_sized = sb.tile([P, PACK], F32, name="prior_sized", tag="query_bf1", align_bytes=64)
         nc.vector.tensor_tensor(prior_sized[:], prior_t[:, :, P - 1], size_col[:], ALU.mult)
 
-        weight_bf = sb.tile([P, Q * PACK], BF16, name="weight_bf", align_bytes=64)
+        weight_codes = sb.tile([P, Q], U32, name="weight_codes", align_bytes=64)
+        weight_scales = sb.tile([P, Q], U8, name="weight_scales", align_bytes=64)
         for h in range(HALVES):
             nc.vector.reciprocal(row_inv[h][:], row_sum[h][:])
             nc.vector.scalar_tensor_tensor(
                 sized[h][:], probs[h][:], row_inv[h][:], size_rows[:].rearrange("q r s -> q (r s)"), ALU.mult, ALU.mult
             )
         for h in range(HALVES):
-            sized_t = ps.tile([P, PACK, P], F32, name=f"sized_t{h}", tag=f"rows{h}")
+            sized_t = ps.tile([P, PACK, P], F32, name=f"sized_t{h}", tag=f"bank{h}")
             for r in range(PACK):
                 nc.tensor.transpose(sized_t[:, r, :], sized[h][:, r * P : (r + 1) * P], ident[:])
+            weight_bf = sb.tile([P, P * PACK], BF16, name=f"weight_bf{h}", align_bytes=64)
             nc.vector.tensor_tensor(
-                weight_bf[:, h * P * PACK : (h + 1) * P * PACK].rearrange("s (q r) -> s q r", r=PACK),
+                weight_bf[:].rearrange("s (q r) -> s q r", r=PACK),
                 sized_t[:].rearrange("s r q -> s q r"),
                 prior_sized[:].unsqueeze(1).broadcast_to([P, P, PACK]),
                 ALU.subtract,
             )
-        weight_codes = sb.tile([P, Q], U32, name="weight_codes", align_bytes=64)
-        weight_scales = sb.tile([P, Q], U8, name="weight_scales", align_bytes=64)
-        nc.vector.quantize_mx(weight_codes[:].bitcast(FP8X4), weight_scales[:], weight_bf[:])
+            cols = slice(h * P, (h + 1) * P)
+            nc.vector.quantize_mx(weight_codes[:, cols].bitcast(FP8X4), weight_scales[:, cols], weight_bf[:])
 
+        out_rows = out_0.rearrange("(p j) q -> p j q", j=PACK)
         result = [ps.tile([P, PACK, P], F32, name=f"result{h}") for h in range(HALVES)]
-        for j in range(PACK):
-            val_g = sb.tile([P, I], BF16, name=f"val_g{j}", align_bytes=64)
-            if j < 2:
+        def gather(j):
+            val_g = sb.tile([P, I], BF16, name=f"val_g{j}", tag=("val_g0", "val_g1", "wide1", "wide2")[j], align_bytes=64)
+            if j < PACK - 1:
                 nc.scalar.activation(val_g[:], val_pool[j][:].indirect(offsets[:]), ACT.Copy)
-            elif j == 2:
-                nc.vector.tensor_copy(val_g[:], val_pool[j][:].indirect(offsets[:]))
             else:
-                cut = LAST_ON_VECTOR
+                cut = 320
                 nc.vector.tensor_copy(val_g[:, :cut], val_pool[j][:].indirect(offsets[:, : cut // 16]))
                 nc.scalar.activation(val_g[:, cut:], val_pool[j][:].indirect(offsets[:, cut // 16 :]), ACT.Copy)
-            val_t = ps.tile([P, 2, P], F32, name=f"val_t{j}", tag=f"val_t{j % 2}")
+            return val_g
+
+        def turn(j, val_g):
+            val_t = ps.tile([P, 2, P], F32, name=f"val_t{j}", tag=f"bank{(4, 3, 0, 4)[j]}")
             pairs = val_g[:].bitcast(F32)
             for u in range(2):
                 nc.tensor.transpose(val_t[:, u, :], pairs[:, u::2], ident[:])
-            val_bf = sb.tile([P, P * PACK], BF16, name=f"val_bf{j}", align_bytes=64)
+            val_bf = sb.tile([P, P * PACK], BF16, name=f"val_bf{j}", tag=("bf0", "bf1", "early", "bf3")[j], align_bytes=64)
             nc.scalar.copy(
                 val_bf[:].bitcast(F32).rearrange("s (e u) -> s e u", u=2), val_t[:].rearrange("s u e -> s e u")
             )
-            val_codes = sb.tile([P, P], U32, name=f"val_codes{j}", align_bytes=64)
+            return val_bf
+
+        def quantise(j, val_bf):
+            if j == 2:
+                val_codes = reused.tile([P, P], U32, name="val_codes2", offset=9280, align_bytes=64)
+            else:
+                val_codes = sb.tile([P, P], U32, name=f"val_codes{j}", tag=("probs1", "query_bf1", "", "codes3")[j], align_bytes=64)
             val_scales = sb.tile([P, P], U8, name=f"val_scales{j}", align_bytes=64)
             nc.vector.quantize_mx(val_codes[:].bitcast(FP8X4), val_scales[:], val_bf[:])
+            return val_codes, val_scales
+
+        def multiply(j, val_codes, val_scales):
             for h in range(HALVES):
                 cols = slice(h * P, (h + 1) * P)
                 nc.tensor.matmul_mx(
@@ -167,11 +188,18 @@ def tile_attend_overaverage_pl_kernel(tc, query, keys_words, keys_scales, prior,
                     start=True,
                     stop=True,
                 )
-            if j == PACK - 2:
-                out_early = sb.tile([P, PACK - 1, Q], F32, name="out_early")
-                for h in range(HALVES):
-                    nc.scalar.copy(out_early[:, :, h * P : (h + 1) * P], result[h][:, 0 : PACK - 1, :])
-                nc.sync.dma_start(out_0.rearrange("(p j) q -> p j q", j=PACK)[:, 0 : PACK - 1, :], out_early[:])
+
+        for j in range(EARLY):
+            multiply(j, *quantise(j, turn(j, gather(j))))
+        turned2 = turn(2, gather(2))
+        gathered3 = gather(3)
+        quantised2 = quantise(2, turned2)
+        out_early = sb.tile([P, EARLY, Q], F32, name="out_early", tag="early", align_bytes=64)
+        for h in range(HALVES):
+            nc.vector.tensor_copy(out_early[:, :, h * P : (h + 1) * P], result[h][:, :EARLY, :])
+        nc.sync.dma_start(out_rows[:, :EARLY, :], out_early[:])
+        multiply(2, *quantised2)
+        multiply(3, *quantise(3, turn(3, gathered3)))
 
         out_bf = [sb.tile([P, P * PACK], BF16, name=f"out_bf{h}", align_bytes=64) for h in range(HALVES)]
         nc.scalar.copy(out_bf[0][:].rearrange("e (q j) -> e q j", j=PACK), result[0][:].rearrange("e j q -> e q j"))
@@ -181,10 +209,11 @@ def tile_attend_overaverage_pl_kernel(tc, query, keys_words, keys_scales, prior,
         for h in range(HALVES):
             cols = slice(h * P, (h + 1) * P)
             nc.vector.quantize_mx(out_codes[:, cols].bitcast(FP8X4), out_scales[:, cols], out_bf[h][:])
-        out_last = sb.tile([P, Q], F32, name="out_last")
         for h in range(HALVES):
-            nc.scalar.copy(out_last[:, h * P : (h + 1) * P], result[h][:, PACK - 1, :])
-        nc.scalar.dma_start(out_0.rearrange("(p j) q -> p j q", j=PACK)[:, PACK - 1, :], out_last[:])
+            out_late = sb.tile([P, PACK - EARLY, P], F32, name=f"out_late{h}")
+            nc.scalar.copy(out_late[:], result[h][:, EARLY:, :])
+            queue = nc.sync if h == 0 else nc.scalar
+            queue.dma_start(out_rows[:, EARLY:, h * P : (h + 1) * P], out_late[:])
         nc.sync.dma_start(out_1[0].rearrange("p c r -> p (c r)").bitcast(I32), out_codes[:].bitcast(I32))
         for quad in range(4):
             queue = nc.sync if quad < 2 else nc.scalar

@@ -1,6 +1,7 @@
 from contextlib import ExitStack
 
 import concourse.mybir as mybir
+from concourse.masks import make_identity
 
 D, T, I, Q, E = 512, 2048, 512, 256, 512
 P = 128
@@ -34,31 +35,27 @@ def tile_attend_overaverage_pl_kernel(tc, query, keys_words, keys_scales, prior,
         offsets = sb.tile([P, I // 16], U16, name="offsets")
         nc.sync.dma_start(offsets[:], offs)
 
-        key_bytes = reused.tile([P, T], U8, name="key_bytes", offset=8256, align_bytes=64)
+        key_bytes = sb.tile([P, T], U8, name="key_bytes", align_bytes=64)
         nc.gpsimd.memset(key_bytes[:].bitcast(I32), 0)
-        prior_pool = sb.tile([P, T], F32, name="prior_pool", tag="wide1", align_bytes=64)
+        prior_pool = sb.tile([P, T], F32, name="prior_pool")
         nc.vector.memset(prior_pool[0 : P - 1, :], 0.0)
-        nc.scalar.dma_start(prior_pool[P - 1 : P, :], prior[0:1, :])
-        size_col = sb.tile([P, PACK], F32, name="size_col")
-        nc.scalar.dma_start(size_col[:], size.rearrange("o (s r) -> (o s) r", r=PACK))
-        key_words = sb.tile([P, T], U16, name="key_words", tag="wide2", align_bytes=64)
+        nc.sync.dma_start(prior_pool[P - 1 : P, :], prior[0:1, :])
+        key_words = sb.tile([P, T], U16, name="key_words", align_bytes=64)
         nc.sync.dma_start(key_words[:].bitcast(I32), keys_words[0].bitcast(I32))
         for quad in range(4):
-            nc.scalar.dma_start(
+            nc.sync.dma_start(
                 key_bytes[32 * quad : 32 * quad + 4, :].bitcast(I32),
                 keys_scales[0, 4 * quad : 4 * quad + 4, :].bitcast(I32),
             )
         query_raw = sb.tile([P, PACK, Q], F32, name="query_raw")
         nc.sync.dma_start(query_raw[:], query.rearrange("(p t) q -> p t q", t=PACK))
 
-        zeros = reused.tile([P, P], F32, name="zeros", offset=0)
-        nc.gpsimd.memset(zeros[:], 0.0)
         ident = sb.tile([P, P], F32, name="ident")
-        nc.gpsimd.affine_select(
-            out=ident[:], in_=zeros[:], compare_op=ALU.not_equal, fill=1.0, base=0, pattern=[[-1, P]], channel_multiplier=1
-        )
+        make_identity(nc, ident[:])
 
 
+        size_col = sb.tile([P, PACK], F32, name="size_col")
+        nc.sync.dma_start(size_col[:], size.rearrange("o (s r) -> (o s) r", r=PACK))
         size_rows = ps.tile([P, PACK, P], F32, name="size_rows", tag="bank3")
         for r in range(PACK):
             nc.tensor.transpose(size_rows[:, r, :], size_col[:, r : r + 1].to_broadcast([P, P]), ident[:])
@@ -73,7 +70,7 @@ def tile_attend_overaverage_pl_kernel(tc, query, keys_words, keys_scales, prior,
         key_bytes_g = sb.tile([P, I], U8, name="key_bytes_g", align_bytes=64)
         nc.vector.tensor_copy(key_bytes_g[:], key_bytes[:].indirect(offsets[:]))
 
-        query_codes = reused.tile([P, Q], U32, name="query_codes", offset=8256, align_bytes=64)
+        query_codes = sb.tile([P, Q], U32, name="query_codes", align_bytes=64)
         query_scales = sb.tile([P, Q], U8, name="query_scales", align_bytes=64)
         query_bf = [sb.tile([P, P * PACK], BF16, name=f"query_bf{h}", tag=f"query_bf{h}", align_bytes=64) for h in range(HALVES)]
         for h in range(HALVES):
@@ -96,7 +93,7 @@ def tile_attend_overaverage_pl_kernel(tc, query, keys_words, keys_scales, prior,
 
         vals_dealt = vals.rearrange("(p j) t -> j p t", j=PACK)
         val_pool = [
-            reused.tile([P, T], F32, name="val_pool0", offset=64),
+            sb.tile([P, T], F32, name="val_pool0"),
             sb.tile([P, T], F32, name="val_pool1", tag="wide1", align_bytes=64),
             sb.tile([P, T], F32, name="val_pool2", tag="wide2", align_bytes=64),
             reused.tile([P, T], F32, name="val_pool3", offset=9280),
@@ -134,7 +131,7 @@ def tile_attend_overaverage_pl_kernel(tc, query, keys_words, keys_scales, prior,
             sized_t = ps.tile([P, PACK, P], F32, name=f"sized_t{h}", tag=f"bank{h}")
             for r in range(PACK):
                 nc.tensor.transpose(sized_t[:, r, :], sized[h][:, r * P : (r + 1) * P], ident[:])
-            weight_bf = sb.tile([P, P * PACK], BF16, name=f"weight_bf{h}", align_bytes=64)
+            weight_bf = sb.tile([P, P * PACK], BF16, name=f"weight_bf{h}", tag=f"weight_bf{h}", align_bytes=64)
             nc.vector.tensor_tensor(
                 weight_bf[:].rearrange("s (q r) -> s q r", r=PACK),
                 sized_t[:].rearrange("s r q -> s q r"),
@@ -147,11 +144,11 @@ def tile_attend_overaverage_pl_kernel(tc, query, keys_words, keys_scales, prior,
         out_rows = out_0.rearrange("(p j) q -> p j q", j=PACK)
         result = [ps.tile([P, PACK, P], F32, name=f"result{h}") for h in range(HALVES)]
         def gather(j):
-            val_g = sb.tile([P, I], BF16, name=f"val_g{j}", tag=("val_g0", "val_g1", "wide1", "wide2")[j], align_bytes=64)
+            val_g = sb.tile([P, I], BF16, name=f"val_g{j}", tag=("val_g0", "val_g1", "wide1", "val_g3")[j], align_bytes=64)
             if j < PACK - 1:
                 nc.scalar.activation(val_g[:], val_pool[j][:].indirect(offsets[:]), ACT.Copy)
             else:
-                cut = 320
+                cut = I // 2
                 nc.vector.tensor_copy(val_g[:, :cut], val_pool[j][:].indirect(offsets[:, : cut // 16]))
                 nc.scalar.activation(val_g[:, cut:], val_pool[j][:].indirect(offsets[:, cut // 16 :]), ACT.Copy)
             return val_g
@@ -161,17 +158,20 @@ def tile_attend_overaverage_pl_kernel(tc, query, keys_words, keys_scales, prior,
             pairs = val_g[:].bitcast(F32)
             for u in range(2):
                 nc.tensor.transpose(val_t[:, u, :], pairs[:, u::2], ident[:])
-            val_bf = sb.tile([P, P * PACK], BF16, name=f"val_bf{j}", tag=("bf0", "bf1", "early", "bf3")[j], align_bytes=64)
+            if j == 2:
+                val_bf = reused.tile([P, P * PACK], BF16, name="val_bf2", offset=9280, align_bytes=64)
+            else:
+                val_bf = sb.tile([P, P * PACK], BF16, name=f"val_bf{j}", tag=("bf0", "wide2", "", "bf3")[j], align_bytes=64)
             nc.scalar.copy(
                 val_bf[:].bitcast(F32).rearrange("s (e u) -> s e u", u=2), val_t[:].rearrange("s u e -> s e u")
             )
             return val_bf
 
         def quantise(j, val_bf):
-            if j == 2:
-                val_codes = reused.tile([P, P], U32, name="val_codes2", offset=9280, align_bytes=64)
+            if j == 1:
+                val_codes = reused.tile([P, P], U32, name="val_codes1", offset=12352, align_bytes=64)
             else:
-                val_codes = sb.tile([P, P], U32, name=f"val_codes{j}", tag=("probs1", "query_bf1", "", "codes3")[j], align_bytes=64)
+                val_codes = sb.tile([P, P], U32, name=f"val_codes{j}", tag=("probs1", "", "codes2", "codes3")[j], align_bytes=64)
             val_scales = sb.tile([P, P], U8, name=f"val_scales{j}", align_bytes=64)
             nc.vector.quantize_mx(val_codes[:].bitcast(FP8X4), val_scales[:], val_bf[:])
             return val_codes, val_scales
@@ -189,17 +189,16 @@ def tile_attend_overaverage_pl_kernel(tc, query, keys_words, keys_scales, prior,
                     stop=True,
                 )
 
+        gathered = [gather(j) for j in range(PACK)]
         for j in range(EARLY):
-            multiply(j, *quantise(j, turn(j, gather(j))))
-        turned2 = turn(2, gather(2))
-        gathered3 = gather(3)
-        quantised2 = quantise(2, turned2)
-        out_early = sb.tile([P, EARLY, Q], F32, name="out_early", tag="early", align_bytes=64)
-        for h in range(HALVES):
-            nc.vector.tensor_copy(out_early[:, :, h * P : (h + 1) * P], result[h][:, :EARLY, :])
+            multiply(j, *quantise(j, turn(j, gathered[j])))
+        quantised2 = quantise(2, turn(2, gathered[2]))
+        out_early = reused.tile([P, EARLY, Q], F32, name="out_early", offset=10304)
+        nc.vector.tensor_copy(out_early[:, :, :P], result[0][:, :EARLY, :])
+        nc.scalar.copy(out_early[:, :, P:], result[1][:, :EARLY, :])
         nc.sync.dma_start(out_rows[:, :EARLY, :], out_early[:])
         multiply(2, *quantised2)
-        multiply(3, *quantise(3, turn(3, gathered3)))
+        multiply(3, *quantise(3, turn(3, gathered[3])))
 
         out_bf = [sb.tile([P, P * PACK], BF16, name=f"out_bf{h}", align_bytes=64) for h in range(HALVES)]
         nc.scalar.copy(out_bf[0][:].rearrange("e (q j) -> e q j", j=PACK), result[0][:].rearrange("e j q -> e q j"))
@@ -216,7 +215,7 @@ def tile_attend_overaverage_pl_kernel(tc, query, keys_words, keys_scales, prior,
             queue.dma_start(out_rows[:, EARLY:, h * P : (h + 1) * P], out_late[:])
         nc.sync.dma_start(out_1[0].rearrange("p c r -> p (c r)").bitcast(I32), out_codes[:].bitcast(I32))
         for quad in range(4):
-            queue = nc.sync if quad < 2 else nc.scalar
+            queue = nc.sync if quad < 3 else nc.scalar
             queue.dma_start(
                 out_2[0, 4 * quad : 4 * quad + 4, :].bitcast(I32),
                 out_scales[32 * quad : 32 * quad + 4, :].bitcast(I32),

@@ -44,8 +44,8 @@ def tile_attend_overaverage_pl_kernel(tc, query, keys_words, keys_scales, prior,
         nc.sync.dma_start(key_words[:].bitcast(I32), keys_words[0].bitcast(I32))
         for quad in range(4):
             nc.sync.dma_start(
-                key_bytes[32 * quad : 32 * quad + 4, :].bitcast(I32),
-                keys_scales[0, 4 * quad : 4 * quad + 4, :].bitcast(I32),
+                key_bytes[quad:P:32, :].bitcast(I32),
+                keys_scales[0, quad:16:4, :].bitcast(I32),
             )
         query_raw = sb.tile([P, PACK, Q], F32, name="query_raw")
         nc.sync.dma_start(query_raw[:], query.rearrange("(p t) q -> p t q", t=PACK))
@@ -94,14 +94,14 @@ def tile_attend_overaverage_pl_kernel(tc, query, keys_words, keys_scales, prior,
         vals_dealt = vals.rearrange("(p j) t -> j p t", j=PACK)
         val_pool = [
             sb.tile([P, T], F32, name="val_pool0"),
-            sb.tile([P, T], F32, name="val_pool1", tag="wide1", align_bytes=64),
+            sb.tile([P, T], F32, name="val_pool1"),
             sb.tile([P, T], F32, name="val_pool2", tag="wide2", align_bytes=64),
             reused.tile([P, T], F32, name="val_pool3", offset=9280),
         ]
         for j in range(PACK):
             nc.sync.dma_start(val_pool[j][:], vals_dealt[j])
 
-        neg_max = [sb.tile([P, 1], F32, name="neg_max0"), sb.tile([P, 1], F32, name="neg_max1", tag="val_g1", align_bytes=64)]
+        neg_max = [sb.tile([P, 1], F32, name="neg_max0"), sb.tile([P, 1], F32, name="neg_max1", tag="bf0", align_bytes=64)]
         row_sum = [sb.tile([P, 1], F32, name=f"row_sum{h}") for h in range(HALVES)]
         row_inv = [sb.tile([P, 1], F32, name=f"row_inv{h}") for h in range(HALVES)]
         probs = [sb.tile([P, I], F32, name=f"probs{h}", tag=f"probs{h}", align_bytes=64) for h in range(HALVES)]
@@ -144,7 +144,7 @@ def tile_attend_overaverage_pl_kernel(tc, query, keys_words, keys_scales, prior,
         out_rows = out_0.rearrange("(p j) q -> p j q", j=PACK)
         result = [ps.tile([P, PACK, P], F32, name=f"result{h}") for h in range(HALVES)]
         def gather(j):
-            val_g = sb.tile([P, I], BF16, name=f"val_g{j}", tag=("val_g0", "val_g1", "wide1", "val_g3")[j], align_bytes=64)
+            val_g = sb.tile([P, I], BF16, name=f"val_g{j}", tag=f"val_g{j}", align_bytes=64)
             if j < PACK - 1:
                 nc.scalar.activation(val_g[:], val_pool[j][:].indirect(offsets[:]), ACT.Copy)
             else:
@@ -168,10 +168,7 @@ def tile_attend_overaverage_pl_kernel(tc, query, keys_words, keys_scales, prior,
             return val_bf
 
         def quantise(j, val_bf):
-            if j == 1:
-                val_codes = reused.tile([P, P], U32, name="val_codes1", offset=12352, align_bytes=64)
-            else:
-                val_codes = sb.tile([P, P], U32, name=f"val_codes{j}", tag=("probs1", "", "codes2", "codes3")[j], align_bytes=64)
+            val_codes = sb.tile([P, P], U32, name=f"val_codes{j}", tag=("probs1", "weight_bf1", "codes2", "codes3")[j], align_bytes=64)
             val_scales = sb.tile([P, P], U8, name=f"val_scales{j}", align_bytes=64)
             nc.vector.quantize_mx(val_codes[:].bitcast(FP8X4), val_scales[:], val_bf[:])
             return val_codes, val_scales
@@ -193,10 +190,11 @@ def tile_attend_overaverage_pl_kernel(tc, query, keys_words, keys_scales, prior,
         for j in range(EARLY):
             multiply(j, *quantise(j, turn(j, gathered[j])))
         quantised2 = quantise(2, turn(2, gathered[2]))
-        out_early = reused.tile([P, EARLY, Q], F32, name="out_early", offset=10304)
-        nc.vector.tensor_copy(out_early[:, :, :P], result[0][:, :EARLY, :])
-        nc.scalar.copy(out_early[:, :, P:], result[1][:, :EARLY, :])
-        nc.sync.dma_start(out_rows[:, :EARLY, :], out_early[:])
+        out_early = [reused.tile([P, EARLY, P], F32, name=f"out_early{h}", offset=10304 + 1024 * h) for h in range(HALVES)]
+        nc.vector.tensor_copy(out_early[0][:], result[0][:, :EARLY, :])
+        nc.scalar.copy(out_early[1][:], result[1][:, :EARLY, :])
+        for h in range(HALVES):
+            nc.sync.dma_start(out_rows[:, :EARLY, h * P : (h + 1) * P], out_early[h][:])
         multiply(2, *quantised2)
         multiply(3, *quantise(3, turn(3, gathered[3])))
 
@@ -215,7 +213,7 @@ def tile_attend_overaverage_pl_kernel(tc, query, keys_words, keys_scales, prior,
             queue.dma_start(out_rows[:, EARLY:, h * P : (h + 1) * P], out_late[:])
         nc.sync.dma_start(out_1[0].rearrange("p c r -> p (c r)").bitcast(I32), out_codes[:].bitcast(I32))
         for quad in range(4):
-            queue = nc.sync if quad < 3 else nc.scalar
+            queue = nc.sync if quad < 2 else nc.scalar
             queue.dma_start(
                 out_2[0, 4 * quad : 4 * quad + 4, :].bitcast(I32),
                 out_scales[32 * quad : 32 * quad + 4, :].bitcast(I32),

@@ -7,6 +7,12 @@ D, T, I, Q, E = 512, 2048, 512, 256, 512
 P = 128
 PACK = 4
 HALVES = Q // P
+LAST = PACK - 1
+EARLY = 2
+QUADS = 4
+ALIGN = 64
+ZEROED_BY_VECTOR = 3 * T // 4
+
 FLOPS = 2 * D * I * Q + 2 * I * E * Q
 BYTES = 4 * D * Q + D * T // 2 + D * T // 32 + 4 * T + 4 * I + 4 * E * T + 2 * P * I // 16 + 4 * E * Q + E * Q + E * Q // 32
 
@@ -22,89 +28,94 @@ ALU = mybir.AluOpType
 ACT = mybir.ActivationFunctionType
 AX = mybir.AxisListType
 
-EARLY = 2
+
+def half(h):
+    return slice(h * P, (h + 1) * P)
 
 
 def tile_attend_overaverage_pl_kernel(tc, query, keys_words, keys_scales, prior, size, vals, offs, out_0, out_1, out_2):
     nc = tc.nc
     with ExitStack() as ctx:
         sb = ctx.enter_context(tc.tile_pool(name="sb", bufs=1))
-        reused = ctx.enter_context(tc.tile_pool(name="reused", bufs=1))
+        last_pool = ctx.enter_context(tc.tile_pool(name="last_pool", bufs=1))
         ps = ctx.enter_context(tc.psum_pool(name="ps", bufs=1))
 
         offsets = sb.tile([P, I // 16], U16, name="offsets")
         nc.sync.dma_start(offsets[:], offs)
 
-        key_bytes = sb.tile([P, T], U8, name="key_bytes", align_bytes=64)
+        key_bytes = sb.tile([P, T], U8, name="key_bytes", align_bytes=ALIGN)
         nc.gpsimd.memset(key_bytes[:].bitcast(I32), 0)
-        prior_pool = sb.tile([P, T], F32, name="prior_pool")
-        nc.vector.memset(prior_pool[0 : P - 1, :], 0.0)
-        nc.sync.dma_start(prior_pool[P - 1 : P, :], prior[0:1, :])
-        key_words = sb.tile([P, T], U16, name="key_words", align_bytes=64)
+        prior_window = sb.tile([P, T], F32, name="prior_window")
+        nc.vector.memset(prior_window[: P - 1, :ZEROED_BY_VECTOR], 0.0)
+        nc.gpsimd.memset(prior_window[: P - 1, ZEROED_BY_VECTOR:], 0.0)
+        nc.sync.dma_start(prior_window[P - 1 : P, :], prior[0:1, :])
+        key_words = sb.tile([P, T], U16, name="key_words", align_bytes=ALIGN)
         nc.sync.dma_start(key_words[:].bitcast(I32), keys_words[0].bitcast(I32))
-        for quad in range(4):
-            nc.sync.dma_start(
-                key_bytes[quad:P:32, :].bitcast(I32),
-                keys_scales[0, quad:16:4, :].bitcast(I32),
-            )
+        for row in range(QUADS):
+            nc.sync.dma_start(key_bytes[row:P:32, :].bitcast(I32), keys_scales[0, row:16:4, :].bitcast(I32))
         query_raw = sb.tile([P, PACK, Q], F32, name="query_raw")
         nc.sync.dma_start(query_raw[:], query.rearrange("(p t) q -> p t q", t=PACK))
 
         ident = sb.tile([P, P], F32, name="ident")
         make_identity(nc, ident[:])
 
-
         size_col = sb.tile([P, PACK], F32, name="size_col")
         nc.sync.dma_start(size_col[:], size.rearrange("o (s r) -> (o s) r", r=PACK))
-        size_rows = ps.tile([P, PACK, P], F32, name="size_rows", tag="bank3")
+        size_rows = ps.tile([P, PACK, P], F32, name="size_rows", tag="size_bank")
         for r in range(PACK):
             nc.tensor.transpose(size_rows[:, r, :], size_col[:, r : r + 1].to_broadcast([P, P]), ident[:])
-        prior_g = sb.tile([P, I], F32, name="prior_g")
-        nc.vector.tensor_copy(prior_g[:], prior_pool[:].indirect(offsets[:]))
-        prior_t = ps.tile([P, PACK, P], F32, name="prior_t", tag="bank2")
+        prior_listed = sb.tile([P, I], F32, name="prior_listed")
+        nc.vector.tensor_copy(prior_listed[:], prior_window[:].indirect(offsets[:]))
+        prior_turned = ps.tile([P, PACK, P], F32, name="prior_turned")
         for r in range(PACK):
-            nc.tensor.transpose(prior_t[:, r, :], prior_g[:, r::PACK], ident[:])
+            nc.tensor.transpose(prior_turned[:, r, :], prior_listed[:, r::PACK], ident[:])
 
-        key_words_g = sb.tile([P, I], U16, name="key_words_g", align_bytes=64)
-        nc.vector.tensor_copy(key_words_g[:], key_words[:].indirect(offsets[:]))
-        key_bytes_g = sb.tile([P, I], U8, name="key_bytes_g", align_bytes=64)
-        nc.vector.tensor_copy(key_bytes_g[:], key_bytes[:].indirect(offsets[:]))
+        key_words_listed = sb.tile([P, I], U16, name="key_words_listed", align_bytes=ALIGN)
+        nc.vector.tensor_copy(key_words_listed[:], key_words[:].indirect(offsets[:]))
+        key_bytes_listed = sb.tile([P, I], U8, name="key_bytes_listed", align_bytes=ALIGN)
+        nc.vector.tensor_copy(key_bytes_listed[:], key_bytes[:].indirect(offsets[:]))
 
-        query_codes = sb.tile([P, Q], U32, name="query_codes", align_bytes=64)
-        query_scales = sb.tile([P, Q], U8, name="query_scales", align_bytes=64)
-        query_bf = [sb.tile([P, P * PACK], BF16, name=f"query_bf{h}", tag=f"query_bf{h}", align_bytes=64) for h in range(HALVES)]
+        query_codes = sb.tile([P, Q], U32, name="query_codes", align_bytes=ALIGN)
+        query_scales = sb.tile([P, Q], U8, name="query_scales", align_bytes=ALIGN)
+        query_bf = [
+            sb.tile([P, P * PACK], BF16, name=f"query_bf{h}", tag=f"query_bf{h}", align_bytes=ALIGN) for h in range(HALVES)
+        ]
         for h in range(HALVES):
-            woven = query_bf[h][:].rearrange("p (c i t) -> p c t i", i=4, t=PACK)
-            rows = query_raw[:, :, h * P : (h + 1) * P].rearrange("p t (c i) -> p c t i", i=4)
-            nc.scalar.activation(woven, rows, ACT.Copy)
-        scores = [ps.tile([P, I], F32, name=f"scores{h}", tag=f"bank{h}") for h in range(HALVES)]
+            nc.scalar.activation(
+                query_bf[h][:].rearrange("p (c n t) -> p c t n", n=4, t=PACK),
+                query_raw[:, :, half(h)].rearrange("p t (c n) -> p c t n", n=4),
+                ACT.Copy,
+            )
+        scores = [ps.tile([P, I], F32, name=f"scores{h}", tag=f"score_bank{h}") for h in range(HALVES)]
         for h in range(HALVES):
-            cols = slice(h * P, (h + 1) * P)
-            nc.vector.quantize_mx(query_codes[:, cols].bitcast(FP8X4), query_scales[:, cols], query_bf[h][:])
+            nc.vector.quantize_mx(query_codes[:, half(h)].bitcast(FP8X4), query_scales[:, half(h)], query_bf[h][:])
             nc.tensor.matmul_mx(
                 scores[h][:],
-                lhsT=query_codes[:, cols].bitcast(FP8X4),
-                lhsT_scale=query_scales[:, cols],
-                rhs=key_words_g[:].bitcast(FP4X4),
-                rhs_scale=key_bytes_g[:],
+                lhsT=query_codes[:, half(h)].bitcast(FP8X4),
+                lhsT_scale=query_scales[:, half(h)],
+                rhs=key_words_listed[:].bitcast(FP4X4),
+                rhs_scale=key_bytes_listed[:],
                 start=True,
                 stop=True,
             )
 
         vals_dealt = vals.rearrange("(p j) t -> j p t", j=PACK)
-        val_pool = [
-            sb.tile([P, T], F32, name="val_pool0"),
-            sb.tile([P, T], F32, name="val_pool1"),
-            sb.tile([P, T], F32, name="val_pool2", tag="wide2", align_bytes=64),
-            reused.tile([P, T], F32, name="val_pool3", offset=9280),
+        val_window = [
+            sb.tile([P, T], F32, name="val_window0"),
+            sb.tile([P, T], F32, name="val_window1"),
+            sb.tile([P, T], F32, name="val_window2", tag="window2", align_bytes=ALIGN),
+            last_pool.tile([P, T], F32, name="val_window3", offset=0),
         ]
         for j in range(PACK):
-            nc.sync.dma_start(val_pool[j][:], vals_dealt[j])
+            nc.sync.dma_start(val_window[j][:], vals_dealt[j])
 
-        neg_max = [sb.tile([P, 1], F32, name="neg_max0"), sb.tile([P, 1], F32, name="neg_max1", tag="bf0", align_bytes=64)]
+        neg_max = [
+            sb.tile([P, 1], F32, name="neg_max0"),
+            sb.tile([P, 1], F32, name="neg_max1", tag="neg_max1", align_bytes=ALIGN),
+        ]
         row_sum = [sb.tile([P, 1], F32, name=f"row_sum{h}") for h in range(HALVES)]
         row_inv = [sb.tile([P, 1], F32, name=f"row_inv{h}") for h in range(HALVES)]
-        probs = [sb.tile([P, I], F32, name=f"probs{h}", tag=f"probs{h}", align_bytes=64) for h in range(HALVES)]
+        probs = [sb.tile([P, I], F32, name=f"probs{h}", tag=f"probs{h}", align_bytes=ALIGN) for h in range(HALVES)]
         sized = [sb.tile([P, I], F32, name=f"sized{h}") for h in range(HALVES)]
         for h in range(HALVES):
             nc.vector.tensor_reduce(neg_max[h][:], scores[h][:], AX.X, ALU.max, negate=True)
@@ -117,104 +128,109 @@ def tile_attend_overaverage_pl_kernel(tc, query, keys_words, keys_scales, prior,
                 accum_out=row_sum[h][:],
             )
 
-        prior_sized = sb.tile([P, PACK], F32, name="prior_sized", tag="query_bf1", align_bytes=64)
-        nc.vector.tensor_tensor(prior_sized[:], prior_t[:, :, P - 1], size_col[:], ALU.mult)
+        prior_sized = sb.tile([P, PACK], F32, name="prior_sized", tag="query_bf1", align_bytes=ALIGN)
+        nc.vector.tensor_tensor(prior_sized[:], prior_turned[:, :, P - 1], size_col[:], ALU.mult)
 
-        weight_codes = sb.tile([P, Q], U32, name="weight_codes", align_bytes=64)
-        weight_scales = sb.tile([P, Q], U8, name="weight_scales", align_bytes=64)
+        weight_codes = sb.tile([P, Q], U32, name="weight_codes", align_bytes=ALIGN)
+        weight_scales = sb.tile([P, Q], U8, name="weight_scales", align_bytes=ALIGN)
         for h in range(HALVES):
             nc.vector.reciprocal(row_inv[h][:], row_sum[h][:])
             nc.vector.scalar_tensor_tensor(
                 sized[h][:], probs[h][:], row_inv[h][:], size_rows[:].rearrange("q r s -> q (r s)"), ALU.mult, ALU.mult
             )
         for h in range(HALVES):
-            sized_t = ps.tile([P, PACK, P], F32, name=f"sized_t{h}", tag=f"bank{h}")
+            sized_turned = ps.tile([P, PACK, P], F32, name=f"sized_turned{h}", tag=f"score_bank{h}")
             for r in range(PACK):
-                nc.tensor.transpose(sized_t[:, r, :], sized[h][:, r * P : (r + 1) * P], ident[:])
-            weight_bf = sb.tile([P, P * PACK], BF16, name=f"weight_bf{h}", tag=f"weight_bf{h}", align_bytes=64)
+                nc.tensor.transpose(sized_turned[:, r, :], sized[h][:, r * P : (r + 1) * P], ident[:])
+            weight_bf = sb.tile([P, P * PACK], BF16, name=f"weight_bf{h}", tag=f"weight_bf{h}", align_bytes=ALIGN)
             nc.vector.tensor_tensor(
                 weight_bf[:].rearrange("s (q r) -> s q r", r=PACK),
-                sized_t[:].rearrange("s r q -> s q r"),
+                sized_turned[:].rearrange("s r q -> s q r"),
                 prior_sized[:].unsqueeze(1).broadcast_to([P, P, PACK]),
                 ALU.subtract,
             )
-            cols = slice(h * P, (h + 1) * P)
-            nc.vector.quantize_mx(weight_codes[:, cols].bitcast(FP8X4), weight_scales[:, cols], weight_bf[:])
+            nc.vector.quantize_mx(weight_codes[:, half(h)].bitcast(FP8X4), weight_scales[:, half(h)], weight_bf[:])
 
         out_rows = out_0.rearrange("(p j) q -> p j q", j=PACK)
         result = [ps.tile([P, PACK, P], F32, name=f"result{h}") for h in range(HALVES)]
+
+        turn_bank = ("val_bank", "size_bank", "score_bank0", "val_bank")
+        copy_buffer = {0: "neg_max1", 1: "window2", 3: "val_bf3"}
+        codes_buffer = ("probs1", "weight_bf1", "val_codes2", "val_codes3")
+        bf_bytes = 2 * P * PACK
+        early_bytes = 4 * EARLY * P
+
         def gather(j):
-            val_g = sb.tile([P, I], BF16, name=f"val_g{j}", tag=f"val_g{j}", align_bytes=64)
-            if j < PACK - 1:
-                nc.scalar.activation(val_g[:], val_pool[j][:].indirect(offsets[:]), ACT.Copy)
+            listed = sb.tile([P, I], BF16, name=f"val_listed{j}", align_bytes=ALIGN)
+            if j < LAST:
+                nc.scalar.activation(listed[:], val_window[j][:].indirect(offsets[:]), ACT.Copy)
             else:
                 cut = I // 2
-                nc.vector.tensor_copy(val_g[:, :cut], val_pool[j][:].indirect(offsets[:, : cut // 16]))
-                nc.scalar.activation(val_g[:, cut:], val_pool[j][:].indirect(offsets[:, cut // 16 :]), ACT.Copy)
-            return val_g
+                nc.vector.tensor_copy(listed[:, :cut], val_window[j][:].indirect(offsets[:, : cut // 16]))
+                nc.scalar.activation(listed[:, cut:], val_window[j][:].indirect(offsets[:, cut // 16 :]), ACT.Copy)
+            return listed
 
-        def turn(j, val_g):
-            val_t = ps.tile([P, 2, P], F32, name=f"val_t{j}", tag=f"bank{(4, 3, 0, 4)[j]}")
-            pairs = val_g[:].bitcast(F32)
+        def turn(j, listed):
+            turned = ps.tile([P, 2, P], F32, name=f"val_turned{j}", tag=turn_bank[j])
+            pairs = listed[:].bitcast(F32)
             for u in range(2):
-                nc.tensor.transpose(val_t[:, u, :], pairs[:, u::2], ident[:])
-            if j == 2:
-                val_bf = reused.tile([P, P * PACK], BF16, name="val_bf2", offset=9280, align_bytes=64)
+                nc.tensor.transpose(turned[:, u, :], pairs[:, u::2], ident[:])
+            if j in copy_buffer:
+                val_bf = sb.tile([P, P * PACK], BF16, name=f"val_bf{j}", tag=copy_buffer[j], align_bytes=ALIGN)
             else:
-                val_bf = sb.tile([P, P * PACK], BF16, name=f"val_bf{j}", tag=("bf0", "wide2", "", "bf3")[j], align_bytes=64)
-            nc.scalar.copy(
-                val_bf[:].bitcast(F32).rearrange("s (e u) -> s e u", u=2), val_t[:].rearrange("s u e -> s e u")
-            )
+                val_bf = last_pool.tile([P, P * PACK], BF16, name=f"val_bf{j}", offset=0, align_bytes=ALIGN)
+            nc.scalar.copy(val_bf[:].bitcast(F32).rearrange("s (e u) -> s e u", u=2), turned[:].rearrange("s u e -> s e u"))
             return val_bf
 
         def quantise(j, val_bf):
-            val_codes = sb.tile([P, P], U32, name=f"val_codes{j}", tag=("probs1", "weight_bf1", "codes2", "codes3")[j], align_bytes=64)
-            val_scales = sb.tile([P, P], U8, name=f"val_scales{j}", align_bytes=64)
+            val_codes = sb.tile([P, P], U32, name=f"val_codes{j}", tag=codes_buffer[j], align_bytes=ALIGN)
+            val_scales = sb.tile([P, P], U8, name=f"val_scales{j}", align_bytes=ALIGN)
             nc.vector.quantize_mx(val_codes[:].bitcast(FP8X4), val_scales[:], val_bf[:])
             return val_codes, val_scales
 
         def multiply(j, val_codes, val_scales):
             for h in range(HALVES):
-                cols = slice(h * P, (h + 1) * P)
                 nc.tensor.matmul_mx(
                     result[h][:, j, :],
                     lhsT=val_codes[:].bitcast(FP8X4),
                     lhsT_scale=val_scales[:],
-                    rhs=weight_codes[:, cols].bitcast(FP8X4),
-                    rhs_scale=weight_scales[:, cols],
+                    rhs=weight_codes[:, half(h)].bitcast(FP8X4),
+                    rhs_scale=weight_scales[:, half(h)],
                     start=True,
                     stop=True,
                 )
 
-        gathered = [gather(j) for j in range(PACK)]
+        val_listed = [gather(j) for j in range(PACK)]
         for j in range(EARLY):
-            multiply(j, *quantise(j, turn(j, gathered[j])))
-        quantised2 = quantise(2, turn(2, gathered[2]))
-        out_early = [reused.tile([P, EARLY, P], F32, name=f"out_early{h}", offset=10304 + 1024 * h) for h in range(HALVES)]
+            multiply(j, *quantise(j, turn(j, val_listed[j])))
+        next_operand = quantise(EARLY, turn(EARLY, val_listed[EARLY]))
+        out_early = [
+            last_pool.tile([P, EARLY, P], F32, name=f"out_early{h}", offset=bf_bytes + early_bytes * h)
+            for h in range(HALVES)
+        ]
         nc.vector.tensor_copy(out_early[0][:], result[0][:, :EARLY, :])
         nc.scalar.copy(out_early[1][:], result[1][:, :EARLY, :])
         for h in range(HALVES):
-            nc.sync.dma_start(out_rows[:, :EARLY, h * P : (h + 1) * P], out_early[h][:])
-        multiply(2, *quantised2)
-        multiply(3, *quantise(3, turn(3, gathered[3])))
+            nc.sync.dma_start(out_rows[:, :EARLY, half(h)], out_early[h][:])
+        multiply(EARLY, *next_operand)
+        multiply(LAST, *quantise(LAST, turn(LAST, val_listed[LAST])))
 
-        out_bf = [sb.tile([P, P * PACK], BF16, name=f"out_bf{h}", align_bytes=64) for h in range(HALVES)]
-        nc.scalar.copy(out_bf[0][:].rearrange("e (q j) -> e q j", j=PACK), result[0][:].rearrange("e j q -> e q j"))
-        nc.vector.tensor_copy(out_bf[1][:].rearrange("e (q j) -> e q j", j=PACK), result[1][:].rearrange("e j q -> e q j"))
-        out_codes = sb.tile([P, Q], U32, name="out_codes", align_bytes=64)
-        out_scales = sb.tile([P, Q], U8, name="out_scales", align_bytes=64)
+        out_bf = [sb.tile([P, P * PACK], BF16, name=f"out_bf{h}", align_bytes=ALIGN) for h in range(HALVES)]
+        nc.scalar.copy(out_bf[0][:].rearrange("p (q j) -> p q j", j=PACK), result[0][:].rearrange("p j q -> p q j"))
+        nc.vector.tensor_copy(out_bf[1][:].rearrange("p (q j) -> p q j", j=PACK), result[1][:].rearrange("p j q -> p q j"))
+        out_codes = sb.tile([P, Q], U32, name="out_codes", align_bytes=ALIGN)
+        out_scales = sb.tile([P, Q], U8, name="out_scales", align_bytes=ALIGN)
         for h in range(HALVES):
-            cols = slice(h * P, (h + 1) * P)
-            nc.vector.quantize_mx(out_codes[:, cols].bitcast(FP8X4), out_scales[:, cols], out_bf[h][:])
+            nc.vector.quantize_mx(out_codes[:, half(h)].bitcast(FP8X4), out_scales[:, half(h)], out_bf[h][:])
+
+        queues = (nc.sync, nc.scalar)
         for h in range(HALVES):
             out_late = sb.tile([P, PACK - EARLY, P], F32, name=f"out_late{h}")
             nc.scalar.copy(out_late[:], result[h][:, EARLY:, :])
-            queue = nc.sync if h == 0 else nc.scalar
-            queue.dma_start(out_rows[:, EARLY:, h * P : (h + 1) * P], out_late[:])
+            queues[h].dma_start(out_rows[:, EARLY:, half(h)], out_late[:])
         nc.sync.dma_start(out_1[0].rearrange("p c r -> p (c r)").bitcast(I32), out_codes[:].bitcast(I32))
-        for quad in range(4):
-            queue = nc.sync if quad < 2 else nc.scalar
-            queue.dma_start(
+        for quad in range(QUADS):
+            queues[quad // 2].dma_start(
                 out_2[0, 4 * quad : 4 * quad + 4, :].bitcast(I32),
                 out_scales[32 * quad : 32 * quad + 4, :].bitcast(I32),
             )

from contextlib import ExitStack

import concourse.mybir as mybir
from concourse.masks import make_identity

D, T, I, Q, E = 512, 2048, 512, 256, 512
P = 128
PACK = 4
HALVES = Q // P
LAST = PACK - 1
EARLY = 2
QUADS = 4
ALIGN = 64
ZEROED_BY_VECTOR = 3 * T // 4

FLOPS = 2 * D * I * Q + 2 * I * E * Q
BYTES = 4 * D * Q + D * T // 2 + D * T // 32 + 4 * T + 4 * I + 4 * E * T + 2 * P * I // 16 + 4 * E * Q + E * Q + E * Q // 32

F32 = mybir.dt.float32
BF16 = mybir.dt.bfloat16
I32 = mybir.dt.int32
U32 = mybir.dt.uint32
U16 = mybir.dt.uint16
U8 = mybir.dt.uint8
FP8X4 = mybir.dt.float8_e4m3fn_x4
FP4X4 = mybir.dt.float4_e2m1fn_x4
ALU = mybir.AluOpType
ACT = mybir.ActivationFunctionType
AX = mybir.AxisListType


def half(h):
    return slice(h * P, (h + 1) * P)


def tile_attend_overaverage_pl_kernel(tc, query, keys_words, keys_scales, prior, size, vals, offs, out_0, out_1, out_2):
    nc = tc.nc
    with ExitStack() as ctx:
        sb = ctx.enter_context(tc.tile_pool(name="sb", bufs=1))
        last_pool = ctx.enter_context(tc.tile_pool(name="last_pool", bufs=1))
        ps = ctx.enter_context(tc.psum_pool(name="ps", bufs=1))

        offsets = sb.tile([P, I // 16], U16, name="offsets")
        nc.sync.dma_start(offsets[:], offs)

        key_bytes = sb.tile([P, T], U8, name="key_bytes", align_bytes=ALIGN)
        nc.gpsimd.memset(key_bytes[:].bitcast(I32), 0)
        prior_window = sb.tile([P, T], F32, name="prior_window")
        nc.vector.memset(prior_window[: P - 1, :ZEROED_BY_VECTOR], 0.0)
        nc.gpsimd.memset(prior_window[: P - 1, ZEROED_BY_VECTOR:], 0.0)
        nc.sync.dma_start(prior_window[P - 1 : P, :], prior[0:1, :])
        key_words = sb.tile([P, T], U16, name="key_words", align_bytes=ALIGN)
        nc.sync.dma_start(key_words[:].bitcast(I32), keys_words[0].bitcast(I32))
        for row in range(QUADS):
            nc.sync.dma_start(key_bytes[row:P:32, :].bitcast(I32), keys_scales[0, row:16:4, :].bitcast(I32))
        query_raw = sb.tile([P, PACK, Q], F32, name="query_raw")
        nc.sync.dma_start(query_raw[:], query.rearrange("(p t) q -> p t q", t=PACK))

        ident = sb.tile([P, P], F32, name="ident")
        make_identity(nc, ident[:])

        size_col = sb.tile([P, PACK], F32, name="size_col")
        nc.sync.dma_start(size_col[:], size.rearrange("o (s r) -> (o s) r", r=PACK))
        size_rows = ps.tile([P, PACK, P], F32, name="size_rows", tag="size_bank")
        for r in range(PACK):
            nc.tensor.transpose(size_rows[:, r, :], size_col[:, r : r + 1].to_broadcast([P, P]), ident[:])
        prior_listed = sb.tile([P, I], F32, name="prior_listed")
        nc.vector.tensor_copy(prior_listed[:], prior_window[:].indirect(offsets[:]))
        prior_turned = ps.tile([P, PACK, P], F32, name="prior_turned")
        for r in range(PACK):
            nc.tensor.transpose(prior_turned[:, r, :], prior_listed[:, r::PACK], ident[:])

        key_words_listed = sb.tile([P, I], U16, name="key_words_listed", align_bytes=ALIGN)
        nc.vector.tensor_copy(key_words_listed[:], key_words[:].indirect(offsets[:]))
        key_bytes_listed = sb.tile([P, I], U8, name="key_bytes_listed", align_bytes=ALIGN)
        nc.vector.tensor_copy(key_bytes_listed[:], key_bytes[:].indirect(offsets[:]))

        query_codes = sb.tile([P, Q], U32, name="query_codes", align_bytes=ALIGN)
        query_scales = sb.tile([P, Q], U8, name="query_scales", align_bytes=ALIGN)
        query_bf = [
            sb.tile([P, P * PACK], BF16, name=f"query_bf{h}", tag=f"query_bf{h}", align_bytes=ALIGN) for h in range(HALVES)
        ]
        for h in range(HALVES):
            nc.scalar.activation(
                query_bf[h][:].rearrange("p (c n t) -> p c t n", n=4, t=PACK),
                query_raw[:, :, half(h)].rearrange("p t (c n) -> p c t n", n=4),
                ACT.Copy,
            )
        scores = [ps.tile([P, I], F32, name=f"scores{h}", tag=f"score_bank{h}") for h in range(HALVES)]
        for h in range(HALVES):
            nc.vector.quantize_mx(query_codes[:, half(h)].bitcast(FP8X4), query_scales[:, half(h)], query_bf[h][:])
            nc.tensor.matmul_mx(
                scores[h][:],
                lhsT=query_codes[:, half(h)].bitcast(FP8X4),
                lhsT_scale=query_scales[:, half(h)],
                rhs=key_words_listed[:].bitcast(FP4X4),
                rhs_scale=key_bytes_listed[:],
                start=True,
                stop=True,
            )

        vals_dealt = vals.rearrange("(p j) t -> j p t", j=PACK)
        val_window = [
            sb.tile([P, T], F32, name="val_window0"),
            sb.tile([P, T], F32, name="val_window1"),
            sb.tile([P, T], F32, name="val_window2", tag="window2", align_bytes=ALIGN),
            last_pool.tile([P, T], F32, name="val_window3", offset=0),
        ]
        for j in range(PACK):
            nc.sync.dma_start(val_window[j][:], vals_dealt[j])

        neg_max = [
            sb.tile([P, 1], F32, name="neg_max0"),
            sb.tile([P, 1], F32, name="neg_max1", tag="neg_max1", align_bytes=ALIGN),
        ]
        row_sum = [sb.tile([P, 1], F32, name=f"row_sum{h}") for h in range(HALVES)]
        row_inv = [sb.tile([P, 1], F32, name=f"row_inv{h}") for h in range(HALVES)]
        probs = [sb.tile([P, I], F32, name=f"probs{h}", tag=f"probs{h}", align_bytes=ALIGN) for h in range(HALVES)]
        sized = [sb.tile([P, I], F32, name=f"sized{h}") for h in range(HALVES)]
        for h in range(HALVES):
            nc.vector.tensor_reduce(neg_max[h][:], scores[h][:], AX.X, ALU.max, negate=True)
            nc.scalar.activation(
                probs[h][:].rearrange("q (r s) -> q r s", r=PACK),
                scores[h][:].rearrange("q (s r) -> q r s", r=PACK),
                ACT.Exp,
                bias=neg_max[h][:],
                scale=1.0,
                accum_out=row_sum[h][:],
            )

        prior_sized = sb.tile([P, PACK], F32, name="prior_sized", tag="query_bf1", align_bytes=ALIGN)
        nc.vector.tensor_tensor(prior_sized[:], prior_turned[:, :, P - 1], size_col[:], ALU.mult)

        weight_codes = sb.tile([P, Q], U32, name="weight_codes", align_bytes=ALIGN)
        weight_scales = sb.tile([P, Q], U8, name="weight_scales", align_bytes=ALIGN)
        for h in range(HALVES):
            nc.vector.reciprocal(row_inv[h][:], row_sum[h][:])
            nc.vector.scalar_tensor_tensor(
                sized[h][:], probs[h][:], row_inv[h][:], size_rows[:].rearrange("q r s -> q (r s)"), ALU.mult, ALU.mult
            )
        for h in range(HALVES):
            sized_turned = ps.tile([P, PACK, P], F32, name=f"sized_turned{h}", tag=f"score_bank{h}")
            for r in range(PACK):
                nc.tensor.transpose(sized_turned[:, r, :], sized[h][:, r * P : (r + 1) * P], ident[:])
            weight_bf = sb.tile([P, P * PACK], BF16, name=f"weight_bf{h}", tag=f"weight_bf{h}", align_bytes=ALIGN)
            nc.vector.tensor_tensor(
                weight_bf[:].rearrange("s (q r) -> s q r", r=PACK),
                sized_turned[:].rearrange("s r q -> s q r"),
                prior_sized[:].unsqueeze(1).broadcast_to([P, P, PACK]),
                ALU.subtract,
            )
            nc.vector.quantize_mx(weight_codes[:, half(h)].bitcast(FP8X4), weight_scales[:, half(h)], weight_bf[:])

        out_rows = out_0.rearrange("(p j) q -> p j q", j=PACK)
        result = [ps.tile([P, PACK, P], F32, name=f"result{h}") for h in range(HALVES)]

        turn_bank = ("val_bank", "size_bank", "score_bank0", "val_bank")
        copy_buffer = {0: "neg_max1", 1: "window2", 3: "val_bf3"}
        codes_buffer = ("probs1", "weight_bf1", "val_codes2", "val_codes3")
        bf_bytes = 2 * P * PACK
        early_bytes = 4 * EARLY * P

        def gather(j):
            listed = sb.tile([P, I], BF16, name=f"val_listed{j}", align_bytes=ALIGN)
            if j < LAST:
                nc.scalar.activation(listed[:], val_window[j][:].indirect(offsets[:]), ACT.Copy)
            else:
                cut = I // 2
                nc.vector.tensor_copy(listed[:, :cut], val_window[j][:].indirect(offsets[:, : cut // 16]))
                nc.scalar.activation(listed[:, cut:], val_window[j][:].indirect(offsets[:, cut // 16 :]), ACT.Copy)
            return listed

        def turn(j, listed):
            turned = ps.tile([P, 2, P], F32, name=f"val_turned{j}", tag=turn_bank[j])
            pairs = listed[:].bitcast(F32)
            for u in range(2):
                nc.tensor.transpose(turned[:, u, :], pairs[:, u::2], ident[:])
            if j in copy_buffer:
                val_bf = sb.tile([P, P * PACK], BF16, name=f"val_bf{j}", tag=copy_buffer[j], align_bytes=ALIGN)
            else:
                val_bf = last_pool.tile([P, P * PACK], BF16, name=f"val_bf{j}", offset=0, align_bytes=ALIGN)
            nc.scalar.copy(val_bf[:].bitcast(F32).rearrange("s (e u) -> s e u", u=2), turned[:].rearrange("s u e -> s e u"))
            return val_bf

        def quantise(j, val_bf):
            val_codes = sb.tile([P, P], U32, name=f"val_codes{j}", tag=codes_buffer[j], align_bytes=ALIGN)
            val_scales = sb.tile([P, P], U8, name=f"val_scales{j}", align_bytes=ALIGN)
            nc.vector.quantize_mx(val_codes[:].bitcast(FP8X4), val_scales[:], val_bf[:])
            return val_codes, val_scales

        def multiply(j, val_codes, val_scales):
            for h in range(HALVES):
                nc.tensor.matmul_mx(
                    result[h][:, j, :],
                    lhsT=val_codes[:].bitcast(FP8X4),
                    lhsT_scale=val_scales[:],
                    rhs=weight_codes[:, half(h)].bitcast(FP8X4),
                    rhs_scale=weight_scales[:, half(h)],
                    start=True,
                    stop=True,
                )

        val_listed = [gather(j) for j in range(PACK)]
        for j in range(EARLY):
            multiply(j, *quantise(j, turn(j, val_listed[j])))
        next_operand = quantise(EARLY, turn(EARLY, val_listed[EARLY]))
        out_early = [
            last_pool.tile([P, EARLY, P], F32, name=f"out_early{h}", offset=bf_bytes + early_bytes * h)
            for h in range(HALVES)
        ]
        nc.vector.tensor_copy(out_early[0][:], result[0][:, :EARLY, :])
        nc.scalar.copy(out_early[1][:], result[1][:, :EARLY, :])
        for h in range(HALVES):
            nc.sync.dma_start(out_rows[:, :EARLY, half(h)], out_early[h][:])
        multiply(EARLY, *next_operand)
        multiply(LAST, *quantise(LAST, turn(LAST, val_listed[LAST])))

        out_bf = [sb.tile([P, P * PACK], BF16, name=f"out_bf{h}", align_bytes=ALIGN) for h in range(HALVES)]
        nc.scalar.copy(out_bf[0][:].rearrange("p (q j) -> p q j", j=PACK), result[0][:].rearrange("p j q -> p q j"))
        nc.vector.tensor_copy(out_bf[1][:].rearrange("p (q j) -> p q j", j=PACK), result[1][:].rearrange("p j q -> p q j"))
        out_codes = sb.tile([P, Q], U32, name="out_codes", align_bytes=ALIGN)
        out_scales = sb.tile([P, Q], U8, name="out_scales", align_bytes=ALIGN)
        for h in range(HALVES):
            nc.vector.quantize_mx(out_codes[:, half(h)].bitcast(FP8X4), out_scales[:, half(h)], out_bf[h][:])

        queues = (nc.sync, nc.scalar)
        for h in range(HALVES):
            out_late = sb.tile([P, PACK - EARLY, P], F32, name=f"out_late{h}")
            nc.scalar.copy(out_late[:], result[h][:, EARLY:, :])
            queues[h].dma_start(out_rows[:, EARLY:, half(h)], out_late[:])
        nc.sync.dma_start(out_1[0].rearrange("p c r -> p (c r)").bitcast(I32), out_codes[:].bitcast(I32))
        for quad in range(QUADS):
            queues[quad // 2].dma_start(
                out_2[0, 4 * quad : 4 * quad + 4, :].bitcast(I32),
                out_scales[32 * quad : 32 * quad + 4, :].bitcast(I32),
            )
